import numpy as np
import ml_dtypes


def mxq(x, axis, fmt="e4m3"):
    dtype, down = {"e4m3": (ml_dtypes.float8_e4m3fn, 7), "e5m2": (ml_dtypes.float8_e5m2, 14)}[fmt]
    v = np.moveaxis(np.asarray(x, np.float32).astype(ml_dtypes.bfloat16).astype(np.float64), axis, -1)
    blocks = v.reshape(v.shape[:-1] + (-1, 32))
    amax = np.abs(blocks).max(-1, keepdims=True)
    byte = np.maximum(np.where(amax > 0, np.frexp(amax)[1] - 1 + 127, 0) - down, 1)
    scale = np.exp2(byte - 127.0)
    codes = (blocks / scale).astype(np.float32).astype(dtype).astype(np.float64)
    return np.moveaxis((codes * scale).reshape(v.shape), -1, axis)


WIDE = False


def mx_kscale(k):
    if not WIDE:
        return np.ones(k)
    levels = np.array([30, -30])
    if k % 512:
        return np.exp2(np.random.permutation(np.resize(levels, k // 32))).repeat(32)
    a = np.empty((k // 512, 16))
    for p in range(k // 512):
        a[p, :8] = np.random.permutation(np.resize(levels, 8))
        for g in range(8):
            far = levels[np.abs(levels - a[p, g]) >= 10]
            a[p, g + 8] = far[np.random.randint(len(far))]
    return np.exp2(a.ravel()).repeat(32)


def f64(x):
    return np.asarray(x).astype(np.float64)


def striped(idx):
    return np.tile(np.asarray(idx).reshape(-1, 16).T, (8, 1)).astype(np.uint16)


def unstriped(offs):
    return offs[:16].T.reshape(-1).astype(np.int64)


def sigmoid(v):
    return 1.0 / (1.0 + np.exp(-v))


def bf(x):
    return np.asarray(x, np.float32).astype(ml_dtypes.bfloat16)


def planes(Y):
    r, m = Y.shape
    b = f64(bf(Y)).reshape(r // 32, 32, m)
    amax = np.abs(b).max(1)
    byte = np.clip(np.where(amax > 0, np.frexp(amax)[1] - 1 + 127 - 7, 1), 1, 254)
    codes = (b * np.exp2(127.0 - byte)[:, None, :]).reshape(r, m).astype(np.float32).astype(ml_dtypes.float8_e4m3fn).view(np.uint8)
    words = codes.reshape(r // 512, 128, 4, m).transpose(0, 1, 3, 2)
    return np.ascontiguousarray(words), np.ascontiguousarray(byte.astype(np.uint8).reshape(r // 512, 16, m))


K, N, T, J = 512, 512, 2048, 512


def setup_inputs():
    n = np.random.standard_normal
    idx = np.random.permutation(T)[:J]
    fj = mx_kscale(J)
    tj = np.ones(T)
    tj[idx] = fj
    return {
        "xt": (n((K, T)) * tj).astype(np.float32),
        "g": (n((N, T)) * np.exp(0.5 * n((1, T))) / tj).astype(np.float32),
        "mom": (1.0 * n((K, N))).astype(np.float32),
        "offs": striped(idx),
    }


def reference(xt, g, mom, offs):
    idx = unstriped(offs)
    xj = f64(xt)[:, idx].T
    gj = f64(g)[:, idx].T
    xjq = mxq(xj, 0, "e4m3")
    gjq = mxq(gj, 0, "e5m2")
    w0 = xjq.T @ gjq
    w = 0.04 * w0
    y = w * sigmoid(2.0 * w * f64(mom))
    words, scales = planes(y)
    return y, words, scales

@@ -1,0 +1,148 @@
+from contextlib import ExitStack
+
+import concourse.mybir as mybir
+from concourse.masks import make_identity
+
+K, N, T, J = 512, 512, 2048, 512
+FLOPS = 2 * K * N * J
+
+F32 = mybir.dt.float32
+BF16 = mybir.dt.bfloat16
+I32 = mybir.dt.int32
+U32 = mybir.dt.uint32
+U16 = mybir.dt.uint16
+U8 = mybir.dt.uint8
+E4M3 = mybir.dt.float8_e4m3fn_x4
+E5M2 = mybir.dt.float8_e5m2_x4
+MULT = mybir.AluOpType.mult
+SIGMOID = mybir.ActivationFunctionType.Sigmoid
+
+P = 128
+PACK = 4
+HALF = N // 2
+
+
+def tile_list_agreeing_update_pl_kernel(tc, xt, g, mom, offs, out_0, out_1, out_2):
+    nc = tc.nc
+    with ExitStack() as ctx:
+        keep = ctx.enter_context(tc.tile_pool(name="keep", bufs=1))
+        ring = ctx.enter_context(tc.tile_pool(name="ring", bufs=2))
+        turn_psum = ctx.enter_context(tc.psum_pool(name="turn", bufs=3))
+        sum_psum = ctx.enter_context(tc.psum_pool(name="sums", bufs=1))
+
+        x_rows = xt.rearrange("(p t) c -> p t c", t=PACK)
+        mom_rows = mom.rearrange("(p t) c -> p t c", t=PACK)
+        y_rows = out_0.rearrange("(p t) c -> p t c", t=PACK)
+        words_out = out_1.rearrange("z p c r -> p (z c r)").bitcast(I32)
+        scales_out = out_2.rearrange("z q c -> q (z c)").bitcast(I32)
+
+        offsets = keep.tile([P, J // 16], U16, name="offsets")
+        g_win = [keep.tile([P, T], F32, name="g_win%d" % s) for s in range(PACK)]
+        x_win = [keep.tile([P, T], F32, name="x_win%d" % t) for t in range(PACK)]
+        mom_sb = [keep.tile([P, 2, N], F32, name="mom%d" % h) for h in range(2)]
+
+        nc.sync.dma_start(g_win[0][:], g[0:P, :])
+        nc.sync.dma_start(offsets[:], offs)
+        for s in range(1, PACK):
+            nc.sync.dma_start(g_win[s][:], g[s * P : (s + 1) * P, :])
+        nc.sync.dma_start(x_win[0][:], x_rows[:, 0, :])
+        nc.sync.dma_start(x_win[1][:], x_rows[:, 1, :])
+        nc.sync.dma_start(mom_sb[0][:], mom_rows[:, 0:2, :])
+        nc.sync.dma_start(x_win[2][:], x_rows[:, 2, :])
+        nc.sync.dma_start(x_win[3][:], x_rows[:, 3, :])
+        nc.sync.dma_start(mom_sb[1][:], mom_rows[:, 2:4, :])
+
+        ident = keep.tile([P, P], F32, name="ident")
+        make_identity(nc, ident[:])
+
+        g_codes = keep.tile([P, N], U32, name="g_codes", align_bytes=64)
+        g_scales = keep.tile([P, N], U8, name="g_scales", align_bytes=64)
+        y = keep.tile([P, PACK, N], F32, name="y")
+        y_codes = keep.tile([P, N], U32, name="y_codes", align_bytes=64)
+        y_scales = keep.tile([P, N], U8, name="y_scales", align_bytes=64)
+
+        def pick(window):
+            picked = ring.tile([P, J], BF16, name="picked", align_bytes=64)
+            nc.vector.tensor_copy(
+                picked[:].rearrange("p (u b e) -> p b u e", u=2, e=16),
+                window[:].indirect(offsets[:]),
+            )
+            turned = turn_psum.tile([P, 2, P], F32, name="turned")
+            pairs = picked[:].bitcast(F32)
+            for u in range(2):
+                nc.tensor.transpose(turned[:, u, :], pairs[:, u * P : (u + 1) * P], ident[:])
+            grouped = ring.tile([P, P * PACK], BF16, name="grouped", align_bytes=64)
+            nc.scalar.copy(
+                grouped[:].bitcast(F32).rearrange("p (c u) -> p c u", u=2),
+                turned[:].rearrange("p u c -> p c u"),
+            )
+            return grouped
+
+        def quantize_g(s, grouped):
+            cols = slice(s * P, (s + 1) * P)
+            nc.vector.quantize_mx(g_codes[:, cols].bitcast(E5M2), g_scales[:, cols], grouped[:])
+
+        def multiply(t, grouped):
+            x_codes = ring.tile([P, P], U32, name="x_codes", align_bytes=64)
+            x_scales = ring.tile([P, P], U8, name="x_scales", align_bytes=64)
+            nc.vector.quantize_mx(x_codes[:].bitcast(E4M3), x_scales[:], grouped[:])
+            w0 = sum_psum.tile([P, N], F32, name="w0_%d" % t)
+            nc.tensor.matmul_mx(
+                out=w0[:],
+                lhsT=x_codes[:].bitcast(E4M3),
+                lhsT_scale=x_scales[:],
+                rhs=g_codes[:].bitcast(E5M2),
+                rhs_scale=g_scales[:],
+                start=True,
+                stop=True,
+            )
+            return w0
+
+        def gate(t, w0, cols):
+            width = cols.stop - cols.start
+            z = ring.tile([P, width], F32, name="z")
+            nc.vector.tensor_tensor(z[:], w0[:, cols], mom_sb[t // 2][:, t % 2, cols], MULT)
+            trust = ring.tile([P, width], F32, name="trust")
+            nc.scalar.activation(trust[:], z[:], SIGMOID, scale=0.08)
+            return trust
+
+        def update(t, w0, trust, cols):
+            nc.vector.scalar_tensor_tensor(y[:, t, cols], w0[:, cols], 0.04, trust[:], MULT, MULT)
+            nc.sync.dma_start(y_rows[:, t, cols], y[:, t, cols])
+
+        def round_y(cols):
+            width = cols.stop - cols.start
+            y_grouped = ring.tile([P, width * PACK], BF16, name="y_grouped", align_bytes=64)
+            nc.vector.tensor_copy(
+                y_grouped[:].rearrange("p (c i t) -> p c t i", t=PACK, i=4),
+                y[:, :, cols].rearrange("p t (c i) -> p c t i", i=4),
+            )
+            return y_grouped
+
+        def quantize_y(cols, y_grouped):
+            nc.vector.quantize_mx(y_codes[:, cols].bitcast(E4M3), y_scales[:, cols], y_grouped[:])
+            nc.sync.dma_start(words_out[:, cols], y_codes[:, cols].bitcast(I32))
+
+        whole = slice(0, N)
+        for s in range(PACK):
+            quantize_g(s, pick(g_win[s]))
+        w0 = [multiply(0, pick(x_win[0]))]
+        for t in range(1, PACK):
+            grouped = pick(x_win[t])
+            trust = gate(t - 1, w0[t - 1], whole)
+            w0.append(multiply(t, grouped))
+            update(t - 1, w0[t - 1], trust, whole)
+
+        halves = [slice(0, HALF), slice(HALF, N)]
+        last = PACK - 1
+        trusts = [gate(last, w0[last], cols) for cols in halves]
+        for cols, trust in zip(halves, trusts):
+            update(last, w0[last], trust, cols)
+        rounded = [round_y(cols) for cols in halves]
+        for cols, y_grouped in zip(halves, rounded):
+            quantize_y(cols, y_grouped)
+        for q in range(4):
+            queue = nc.scalar if q % 2 else nc.sync
+            queue.dma_start(
+                scales_out[4 * q : 4 * q + 4, :], y_scales[32 * q : 32 * q + 4, :].bitcast(I32)
+            )

@@ -26,9 +26,11 @@ def tile_list_agreeing_update_pl_kernel(tc, xt, g, mom, offs, out_0, out_1, out_
     nc = tc.nc
     with ExitStack() as ctx:
         keep = ctx.enter_context(tc.tile_pool(name="keep", bufs=1))
-        ring = ctx.enter_context(tc.tile_pool(name="ring", bufs=2))
         turn_psum = ctx.enter_context(tc.psum_pool(name="turn", bufs=3))
         sum_psum = ctx.enter_context(tc.psum_pool(name="sums", bufs=1))
+
+        def tile(name, shape, dtype, place=None):
+            return keep.tile(shape, dtype, name=name, tag=place or name, align_bytes=64)
 
         x_rows = xt.rearrange("(p t) c -> p t c", t=PACK)
         mom_rows = mom.rearrange("(p t) c -> p t c", t=PACK)
@@ -37,32 +39,33 @@ def tile_list_agreeing_update_pl_kernel(tc, xt, g, mom, offs, out_0, out_1, out_
         scales_out = out_2.rearrange("z q c -> q (z c)").bitcast(I32)
 
         offsets = keep.tile([P, J // 16], U16, name="offsets")
-        g_win = [keep.tile([P, T], F32, name="g_win%d" % s) for s in range(PACK)]
-        x_win = [keep.tile([P, T], F32, name="x_win%d" % t) for t in range(PACK)]
-        mom_sb = [keep.tile([P, 2, N], F32, name="mom%d" % h) for h in range(2)]
+        g_win = [tile("g_win%d" % s, [P, T], F32) for s in range(PACK)]
+        x_win = [tile("x_win%d" % t, [P, T], F32) for t in range(PACK)]
+        mom01 = tile("mom01", [P, 2, N], F32)
+        mom2 = tile("mom2", [P, N], F32)
+        mom3 = tile("mom3", [P, N], F32)
+        mom_sb = [mom01[:, 0, :], mom01[:, 1, :], mom2[:], mom3[:]]
 
         nc.sync.dma_start(g_win[0][:], g[0:P, :])
         nc.sync.dma_start(offsets[:], offs)
         for s in range(1, PACK):
             nc.sync.dma_start(g_win[s][:], g[s * P : (s + 1) * P, :])
-        nc.sync.dma_start(x_win[0][:], x_rows[:, 0, :])
-        nc.sync.dma_start(x_win[1][:], x_rows[:, 1, :])
-        nc.sync.dma_start(mom_sb[0][:], mom_rows[:, 0:2, :])
-        nc.sync.dma_start(x_win[2][:], x_rows[:, 2, :])
-        nc.sync.dma_start(x_win[3][:], x_rows[:, 3, :])
-        nc.sync.dma_start(mom_sb[1][:], mom_rows[:, 2:4, :])
+        for t in range(PACK):
+            nc.sync.dma_start(x_win[t][:], x_rows[:, t, :])
+        nc.sync.dma_start(mom01[:], mom_rows[:, 0:2, :])
+        nc.sync.dma_start(mom2[:], mom_rows[:, 2, :])
+        nc.sync.dma_start(mom3[:], mom_rows[:, 3, :])
 
         ident = keep.tile([P, P], F32, name="ident")
         make_identity(nc, ident[:])
+        warm = keep.tile([P, 1], F32, name="warm")
+        nc.scalar.activation(warm[:], ident[:, 0:1], SIGMOID)
 
-        g_codes = keep.tile([P, N], U32, name="g_codes", align_bytes=64)
-        g_scales = keep.tile([P, N], U8, name="g_scales", align_bytes=64)
-        y = keep.tile([P, PACK, N], F32, name="y")
-        y_codes = keep.tile([P, N], U32, name="y_codes", align_bytes=64)
-        y_scales = keep.tile([P, N], U8, name="y_scales", align_bytes=64)
+        y_codes = tile("y_codes", [P, N], U32)
+        y_scales = tile("y_scales", [P, N], U8)
 
-        def pick(window):
-            picked = ring.tile([P, J], BF16, name="picked", align_bytes=64)
+        def pick(name, window, grouped):
+            picked = tile("picked_" + name, [P, J], BF16)
             nc.vector.tensor_copy(
                 picked[:].rearrange("p (u b e) -> p b u e", u=2, e=16),
                 window[:].indirect(offsets[:]),
@@ -71,24 +74,24 @@ def tile_list_agreeing_update_pl_kernel(tc, xt, g, mom, offs, out_0, out_1, out_
             pairs = picked[:].bitcast(F32)
             for u in range(2):
                 nc.tensor.transpose(turned[:, u, :], pairs[:, u * P : (u + 1) * P], ident[:])
-            grouped = ring.tile([P, P * PACK], BF16, name="grouped", align_bytes=64)
             nc.scalar.copy(
-                grouped[:].bitcast(F32).rearrange("p (c u) -> p c u", u=2),
+                grouped.bitcast(F32).rearrange("p (c u) -> p c u", u=2),
                 turned[:].rearrange("p u c -> p c u"),
             )
-            return grouped
 
-        def quantize_g(s, grouped):
-            cols = slice(s * P, (s + 1) * P)
-            nc.vector.quantize_mx(g_codes[:, cols].bitcast(E5M2), g_scales[:, cols], grouped[:])
+        x_grouped = [tile("x_grouped%d" % t, [P, P * PACK], BF16) for t in range(PACK)]
 
-        def multiply(t, grouped):
-            x_codes = ring.tile([P, P], U32, name="x_codes", align_bytes=64)
-            x_scales = ring.tile([P, P], U8, name="x_scales", align_bytes=64)
-            nc.vector.quantize_mx(x_codes[:].bitcast(E4M3), x_scales[:], grouped[:])
-            w0 = sum_psum.tile([P, N], F32, name="w0_%d" % t)
+        def pick_x(t):
+            pick("x%d" % t, x_win[t], x_grouped[t][:])
+
+        w0 = [sum_psum.tile([P, N], F32, name="w0_%d" % t) for t in range(PACK)]
+
+        def multiply(t, place=None):
+            x_codes = tile("x_codes%d" % t, [P, P], U32, place)
+            x_scales = tile("x_scales%d" % t, [P, P], U8)
+            nc.vector.quantize_mx(x_codes[:].bitcast(E4M3), x_scales[:], x_grouped[t][:])
             nc.tensor.matmul_mx(
-                out=w0[:],
+                out=w0[t][:],
                 lhsT=x_codes[:].bitcast(E4M3),
                 lhsT_scale=x_scales[:],
                 rhs=g_codes[:].bitcast(E5M2),
@@ -96,23 +99,23 @@ def tile_list_agreeing_update_pl_kernel(tc, xt, g, mom, offs, out_0, out_1, out_
                 start=True,
                 stop=True,
             )
-            return w0
 
-        def gate(t, w0, cols):
+        def gate(t, cols, place=None):
             width = cols.stop - cols.start
-            z = ring.tile([P, width], F32, name="z")
-            nc.vector.tensor_tensor(z[:], w0[:, cols], mom_sb[t // 2][:, t % 2, cols], MULT)
-            trust = ring.tile([P, width], F32, name="trust")
+            name = "%d_%d" % (t, cols.start)
+            z = tile("z" + name, [P, width], F32, place)
+            nc.vector.tensor_tensor(z[:], w0[t][:, cols], mom_sb[t][:, cols], MULT)
+            trust = tile("trust" + name, [P, width], F32)
             nc.scalar.activation(trust[:], z[:], SIGMOID, scale=0.08)
             return trust
 
-        def update(t, w0, trust, cols):
-            nc.vector.scalar_tensor_tensor(y[:, t, cols], w0[:, cols], 0.04, trust[:], MULT, MULT)
+        def update(t, trust, cols):
+            nc.vector.scalar_tensor_tensor(y[:, t, cols], w0[t][:, cols], 0.04, trust[:], MULT, MULT)
             nc.sync.dma_start(y_rows[:, t, cols], y[:, t, cols])
 
         def round_y(cols):
             width = cols.stop - cols.start
-            y_grouped = ring.tile([P, width * PACK], BF16, name="y_grouped", align_bytes=64)
+            y_grouped = tile("y_grouped%d" % cols.start, [P, width * PACK], BF16)
             nc.vector.tensor_copy(
                 y_grouped[:].rearrange("p (c i t) -> p c t i", t=PACK, i=4),
                 y[:, :, cols].rearrange("p t (c i) -> p c t i", i=4),
@@ -124,20 +127,30 @@ def tile_list_agreeing_update_pl_kernel(tc, xt, g, mom, offs, out_0, out_1, out_
             nc.sync.dma_start(words_out[:, cols], y_codes[:, cols].bitcast(I32))
 
         whole = slice(0, N)
+        g_grouped = tile("g_grouped", [P, N * PACK], BF16)
         for s in range(PACK):
-            quantize_g(s, pick(g_win[s]))
-        w0 = [multiply(0, pick(x_win[0]))]
+            pick("g%d" % s, g_win[s], g_grouped[:, s * P * PACK : (s + 1) * P * PACK])
+        pick_x(0)
+        g_codes = tile("g_codes", [P, N], U32, "x_win0")
+        g_scales = tile("g_scales", [P, N], U8)
+        nc.vector.quantize_mx(g_codes[:].bitcast(E5M2), g_scales[:], g_grouped[:])
         for t in range(1, PACK):
-            grouped = pick(x_win[t])
-            trust = gate(t - 1, w0[t - 1], whole)
-            w0.append(multiply(t, grouped))
-            update(t - 1, w0[t - 1], trust, whole)
+            pick_x(t)
+            multiply(t - 1, "x_win%d" % t)
+        y = tile("y", [P, PACK, N], F32)
+        trust0 = gate(0, whole)
+        trust1 = gate(1, whole)
+        trust2 = gate(2, whole)
+        multiply(3, "mom01")
+        update(0, trust0, whole)
+        update(1, trust1, whole)
 
         halves = [slice(0, HALF), slice(HALF, N)]
         last = PACK - 1
-        trusts = [gate(last, w0[last], cols) for cols in halves]
+        trusts = [gate(last, cols) for cols in halves]
+        update(2, trust2, whole)
         for cols, trust in zip(halves, trusts):
-            update(last, w0[last], trust, cols)
+            update(last, trust, cols)
         rounded = [round_y(cols) for cols in halves]
         for cols, y_grouped in zip(halves, rounded):
             quantize_y(cols, y_grouped)

@@ -20,6 +20,7 @@ SIGMOID = mybir.ActivationFunctionType.Sigmoid
 P = 128
 PACK = 4
 HALF = N // 2
+QUARTER = N // 4
 
 
 def tile_list_agreeing_update_pl_kernel(tc, xt, g, mom, offs, out_0, out_1, out_2):
@@ -33,23 +34,23 @@ def tile_list_agreeing_update_pl_kernel(tc, xt, g, mom, offs, out_0, out_1, out_
             return keep.tile(shape, dtype, name=name, tag=place or name, align_bytes=64)
 
         x_rows = xt.rearrange("(p t) c -> p t c", t=PACK)
+        g_rows = g.rearrange("(h p s) c -> h p s c", h=2, s=2)
         mom_rows = mom.rearrange("(p t) c -> p t c", t=PACK)
         y_rows = out_0.rearrange("(p t) c -> p t c", t=PACK)
         words_out = out_1.rearrange("z p c r -> p (z c r)").bitcast(I32)
         scales_out = out_2.rearrange("z q c -> q (z c)").bitcast(I32)
 
         offsets = keep.tile([P, J // 16], U16, name="offsets")
-        g_win = [tile("g_win%d" % s, [P, T], F32) for s in range(PACK)]
+        g_win = [tile("g_win%d" % h, [P, 2, T], F32) for h in range(2)]
         x_win = [tile("x_win%d" % t, [P, T], F32) for t in range(PACK)]
         mom01 = tile("mom01", [P, 2, N], F32)
         mom2 = tile("mom2", [P, N], F32)
         mom3 = tile("mom3", [P, N], F32)
         mom_sb = [mom01[:, 0, :], mom01[:, 1, :], mom2[:], mom3[:]]
 
-        nc.sync.dma_start(g_win[0][:], g[0:P, :])
+        nc.sync.dma_start(g_win[0][:], g_rows[0])
         nc.sync.dma_start(offsets[:], offs)
-        for s in range(1, PACK):
-            nc.sync.dma_start(g_win[s][:], g[s * P : (s + 1) * P, :])
+        nc.sync.dma_start(g_win[1][:], g_rows[1])
         for t in range(PACK):
             nc.sync.dma_start(x_win[t][:], x_rows[:, t, :])
         nc.sync.dma_start(mom01[:], mom_rows[:, 0:2, :])
@@ -61,32 +62,41 @@ def tile_list_agreeing_update_pl_kernel(tc, xt, g, mom, offs, out_0, out_1, out_
         warm = keep.tile([P, 1], F32, name="warm")
         nc.scalar.activation(warm[:], ident[:, 0:1], SIGMOID)
 
-        y_codes = tile("y_codes", [P, N], U32)
-        y_scales = tile("y_scales", [P, N], U8)
-
-        def pick(name, window, grouped):
+        def pick(name, window, turned):
             picked = tile("picked_" + name, [P, J], BF16)
             nc.vector.tensor_copy(
                 picked[:].rearrange("p (u b e) -> p b u e", u=2, e=16),
-                window[:].indirect(offsets[:]),
+                window.indirect(offsets[:]),
             )
-            turned = turn_psum.tile([P, 2, P], F32, name="turned")
             pairs = picked[:].bitcast(F32)
             for u in range(2):
                 nc.tensor.transpose(turned[:, u, :], pairs[:, u * P : (u + 1) * P], ident[:])
+
+        g_grouped = tile("g_grouped", [P, N * PACK], BF16)
+
+        def pick_g(h):
+            turned = turn_psum.tile([P, 2, 2, P], F32, name="turned")
+            for s in range(2):
+                pick("g%d%d" % (h, s), g_win[h][:, s, :], turned[:, s, :, :])
+            words = g_grouped[:, h * HALF * PACK : (h + 1) * HALF * PACK].bitcast(F32)
             nc.scalar.copy(
-                grouped.bitcast(F32).rearrange("p (c u) -> p c u", u=2),
-                turned[:].rearrange("p u c -> p c u"),
+                words.rearrange("p (c s u) -> p c s u", s=2, u=2),
+                turned[:].rearrange("p s u c -> p c s u"),
             )
 
         x_grouped = [tile("x_grouped%d" % t, [P, P * PACK], BF16) for t in range(PACK)]
 
         def pick_x(t):
-            pick("x%d" % t, x_win[t], x_grouped[t][:])
+            turned = turn_psum.tile([P, 2, P], F32, name="turned")
+            pick("x%d" % t, x_win[t][:], turned)
+            nc.scalar.copy(
+                x_grouped[t][:].bitcast(F32).rearrange("p (c u) -> p c u", u=2),
+                turned[:].rearrange("p u c -> p c u"),
+            )
 
         w0 = [sum_psum.tile([P, N], F32, name="w0_%d" % t) for t in range(PACK)]
 
-        def multiply(t, place=None):
+        def multiply(t, place):
             x_codes = tile("x_codes%d" % t, [P, P], U32, place)
             x_scales = tile("x_scales%d" % t, [P, P], U8)
             nc.vector.quantize_mx(x_codes[:].bitcast(E4M3), x_scales[:], x_grouped[t][:])
@@ -100,36 +110,41 @@ def tile_list_agreeing_update_pl_kernel(tc, xt, g, mom, offs, out_0, out_1, out_
                 stop=True,
             )
 
-        def gate(t, cols, place=None):
+        def gate(t, cols):
             width = cols.stop - cols.start
             name = "%d_%d" % (t, cols.start)
-            z = tile("z" + name, [P, width], F32, place)
+            z = tile("z" + name, [P, width], F32)
             nc.vector.tensor_tensor(z[:], w0[t][:, cols], mom_sb[t][:, cols], MULT)
             trust = tile("trust" + name, [P, width], F32)
             nc.scalar.activation(trust[:], z[:], SIGMOID, scale=0.08)
             return trust
 
+        y = tile("y", [P, PACK, N], F32)
+
         def update(t, trust, cols):
             nc.vector.scalar_tensor_tensor(y[:, t, cols], w0[t][:, cols], 0.04, trust[:], MULT, MULT)
-            nc.sync.dma_start(y_rows[:, t, cols], y[:, t, cols])
 
-        def round_y(cols):
-            width = cols.stop - cols.start
-            y_grouped = tile("y_grouped%d" % cols.start, [P, width * PACK], BF16)
-            nc.vector.tensor_copy(
-                y_grouped[:].rearrange("p (c i t) -> p c t i", t=PACK, i=4),
+        y_grouped = tile("y_grouped", [P, N * PACK], BF16)
+        y_codes = tile("y_codes", [P, N], U32)
+        y_scales = tile("y_scales", [P, N], U8)
+
+        def round_y(copy, cols):
+            copy(
+                y_grouped[:, cols.start * PACK : cols.stop * PACK].rearrange("p (c i t) -> p c t i", t=PACK, i=4),
                 y[:, :, cols].rearrange("p t (c i) -> p c t i", i=4),
             )
-            return y_grouped
 
-        def quantize_y(cols, y_grouped):
-            nc.vector.quantize_mx(y_codes[:, cols].bitcast(E4M3), y_scales[:, cols], y_grouped[:])
+        def quantize_y(cols):
+            nc.vector.quantize_mx(
+                y_codes[:, cols].bitcast(E4M3),
+                y_scales[:, cols],
+                y_grouped[:, cols.start * PACK : cols.stop * PACK],
+            )
             nc.sync.dma_start(words_out[:, cols], y_codes[:, cols].bitcast(I32))
 
         whole = slice(0, N)
-        g_grouped = tile("g_grouped", [P, N * PACK], BF16)
-        for s in range(PACK):
-            pick("g%d" % s, g_win[s], g_grouped[:, s * P * PACK : (s + 1) * P * PACK])
+        for h in range(2):
+            pick_g(h)
         pick_x(0)
         g_codes = tile("g_codes", [P, N], U32, "x_win0")
         g_scales = tile("g_scales", [P, N], U8)
@@ -137,23 +152,28 @@ def tile_list_agreeing_update_pl_kernel(tc, xt, g, mom, offs, out_0, out_1, out_
         for t in range(1, PACK):
             pick_x(t)
             multiply(t - 1, "x_win%d" % t)
-        y = tile("y", [P, PACK, N], F32)
         trust0 = gate(0, whole)
         trust1 = gate(1, whole)
         trust2 = gate(2, whole)
         multiply(3, "mom01")
         update(0, trust0, whole)
+        nc.sync.dma_start(y_rows[:, 0, :], y[:, 0, :])
         update(1, trust1, whole)
+        nc.sync.dma_start(y_rows[:, 1, :], y[:, 1, :])
 
         halves = [slice(0, HALF), slice(HALF, N)]
         last = PACK - 1
         trusts = [gate(last, cols) for cols in halves]
         update(2, trust2, whole)
+        nc.sync.dma_start(y_rows[:, 2, :], y[:, 2, :])
         for cols, trust in zip(halves, trusts):
             update(last, trust, cols)
-        rounded = [round_y(cols) for cols in halves]
-        for cols, y_grouped in zip(halves, rounded):
-            quantize_y(cols, y_grouped)
+        nc.sync.dma_start(y_rows[:, 3, :], y[:, 3, :])
+        round_y(nc.scalar.copy, slice(0, QUARTER))
+        round_y(nc.vector.tensor_copy, slice(QUARTER, HALF))
+        round_y(nc.vector.tensor_copy, slice(HALF, N))
+        for cols in halves:
+            quantize_y(cols)
         for q in range(4):
             queue = nc.scalar if q % 2 else nc.sync
             queue.dma_start(

from contextlib import ExitStack

import concourse.mybir as mybir
from concourse.masks import make_identity

K, N, T, J = 512, 512, 2048, 512
FLOPS = 2 * K * N * J

F32 = mybir.dt.float32
BF16 = mybir.dt.bfloat16
I32 = mybir.dt.int32
U32 = mybir.dt.uint32
U16 = mybir.dt.uint16
U8 = mybir.dt.uint8
E4M3 = mybir.dt.float8_e4m3fn_x4
E5M2 = mybir.dt.float8_e5m2_x4
MULT = mybir.AluOpType.mult
SIGMOID = mybir.ActivationFunctionType.Sigmoid

P = 128
PACK = 4
HALF = N // 2
QUARTER = N // 4


def tile_list_agreeing_update_pl_kernel(tc, xt, g, mom, offs, out_0, out_1, out_2):
    nc = tc.nc
    with ExitStack() as ctx:
        keep = ctx.enter_context(tc.tile_pool(name="keep", bufs=1))
        turn_psum = ctx.enter_context(tc.psum_pool(name="turn", bufs=3))
        sum_psum = ctx.enter_context(tc.psum_pool(name="sums", bufs=1))

        def tile(name, shape, dtype, place=None):
            return keep.tile(shape, dtype, name=name, tag=place or name, align_bytes=64)

        x_rows = xt.rearrange("(p t) c -> p t c", t=PACK)
        g_rows = g.rearrange("(h p s) c -> h p s c", h=2, s=2)
        mom_rows = mom.rearrange("(p t) c -> p t c", t=PACK)
        y_rows = out_0.rearrange("(p t) c -> p t c", t=PACK)
        words_out = out_1.rearrange("z p c r -> p (z c r)").bitcast(I32)
        scales_out = out_2.rearrange("z q c -> q (z c)").bitcast(I32)

        offsets = keep.tile([P, J // 16], U16, name="offsets")
        g_win = [tile("g_win%d" % h, [P, 2, T], F32) for h in range(2)]
        x_win = [tile("x_win%d" % t, [P, T], F32) for t in range(PACK)]
        mom01 = tile("mom01", [P, 2, N], F32)
        mom2 = tile("mom2", [P, N], F32)
        mom3 = tile("mom3", [P, N], F32)
        mom_sb = [mom01[:, 0, :], mom01[:, 1, :], mom2[:], mom3[:]]

        nc.sync.dma_start(g_win[0][:], g_rows[0])
        nc.sync.dma_start(offsets[:], offs)
        nc.sync.dma_start(g_win[1][:], g_rows[1])
        for t in range(PACK):
            nc.sync.dma_start(x_win[t][:], x_rows[:, t, :])
        nc.sync.dma_start(mom01[:], mom_rows[:, 0:2, :])
        nc.sync.dma_start(mom2[:], mom_rows[:, 2, :])
        nc.sync.dma_start(mom3[:], mom_rows[:, 3, :])

        ident = keep.tile([P, P], F32, name="ident")
        make_identity(nc, ident[:])
        warm = keep.tile([P, 1], F32, name="warm")
        nc.scalar.activation(warm[:], ident[:, 0:1], SIGMOID)

        def pick(name, window, turned):
            picked = tile("picked_" + name, [P, J], BF16)
            nc.vector.tensor_copy(
                picked[:].rearrange("p (u b e) -> p b u e", u=2, e=16),
                window.indirect(offsets[:]),
            )
            pairs = picked[:].bitcast(F32)
            for u in range(2):
                nc.tensor.transpose(turned[:, u, :], pairs[:, u * P : (u + 1) * P], ident[:])

        g_grouped = tile("g_grouped", [P, N * PACK], BF16)

        def pick_g(h):
            turned = turn_psum.tile([P, 2, 2, P], F32, name="turned")
            for s in range(2):
                pick("g%d%d" % (h, s), g_win[h][:, s, :], turned[:, s, :, :])
            words = g_grouped[:, h * HALF * PACK : (h + 1) * HALF * PACK].bitcast(F32)
            nc.scalar.copy(
                words.rearrange("p (c s u) -> p c s u", s=2, u=2),
                turned[:].rearrange("p s u c -> p c s u"),
            )

        x_grouped = [tile("x_grouped%d" % t, [P, P * PACK], BF16) for t in range(PACK)]

        def pick_x(t):
            turned = turn_psum.tile([P, 2, P], F32, name="turned")
            pick("x%d" % t, x_win[t][:], turned)
            nc.scalar.copy(
                x_grouped[t][:].bitcast(F32).rearrange("p (c u) -> p c u", u=2),
                turned[:].rearrange("p u c -> p c u"),
            )

        w0 = [sum_psum.tile([P, N], F32, name="w0_%d" % t) for t in range(PACK)]

        def multiply(t, place):
            x_codes = tile("x_codes%d" % t, [P, P], U32, place)
            x_scales = tile("x_scales%d" % t, [P, P], U8)
            nc.vector.quantize_mx(x_codes[:].bitcast(E4M3), x_scales[:], x_grouped[t][:])
            nc.tensor.matmul_mx(
                out=w0[t][:],
                lhsT=x_codes[:].bitcast(E4M3),
                lhsT_scale=x_scales[:],
                rhs=g_codes[:].bitcast(E5M2),
                rhs_scale=g_scales[:],
                start=True,
                stop=True,
            )

        def gate(t, cols):
            width = cols.stop - cols.start
            name = "%d_%d" % (t, cols.start)
            z = tile("z" + name, [P, width], F32)
            nc.vector.tensor_tensor(z[:], w0[t][:, cols], mom_sb[t][:, cols], MULT)
            trust = tile("trust" + name, [P, width], F32)
            nc.scalar.activation(trust[:], z[:], SIGMOID, scale=0.08)
            return trust

        y = tile("y", [P, PACK, N], F32)

        def update(t, trust, cols):
            nc.vector.scalar_tensor_tensor(y[:, t, cols], w0[t][:, cols], 0.04, trust[:], MULT, MULT)

        y_grouped = tile("y_grouped", [P, N * PACK], BF16)
        y_codes = tile("y_codes", [P, N], U32)
        y_scales = tile("y_scales", [P, N], U8)

        def round_y(copy, cols):
            copy(
                y_grouped[:, cols.start * PACK : cols.stop * PACK].rearrange("p (c i t) -> p c t i", t=PACK, i=4),
                y[:, :, cols].rearrange("p t (c i) -> p c t i", i=4),
            )

        def quantize_y(cols):
            nc.vector.quantize_mx(
                y_codes[:, cols].bitcast(E4M3),
                y_scales[:, cols],
                y_grouped[:, cols.start * PACK : cols.stop * PACK],
            )
            nc.sync.dma_start(words_out[:, cols], y_codes[:, cols].bitcast(I32))

        whole = slice(0, N)
        for h in range(2):
            pick_g(h)
        pick_x(0)
        g_codes = tile("g_codes", [P, N], U32, "x_win0")
        g_scales = tile("g_scales", [P, N], U8)
        nc.vector.quantize_mx(g_codes[:].bitcast(E5M2), g_scales[:], g_grouped[:])
        for t in range(1, PACK):
            pick_x(t)
            multiply(t - 1, "x_win%d" % t)
        trust0 = gate(0, whole)
        trust1 = gate(1, whole)
        trust2 = gate(2, whole)
        multiply(3, "mom01")
        update(0, trust0, whole)
        nc.sync.dma_start(y_rows[:, 0, :], y[:, 0, :])
        update(1, trust1, whole)
        nc.sync.dma_start(y_rows[:, 1, :], y[:, 1, :])

        halves = [slice(0, HALF), slice(HALF, N)]
        last = PACK - 1
        trusts = [gate(last, cols) for cols in halves]
        update(2, trust2, whole)
        nc.sync.dma_start(y_rows[:, 2, :], y[:, 2, :])
        for cols, trust in zip(halves, trusts):
            update(last, trust, cols)
        nc.sync.dma_start(y_rows[:, 3, :], y[:, 3, :])
        round_y(nc.scalar.copy, slice(0, QUARTER))
        round_y(nc.vector.tensor_copy, slice(QUARTER, HALF))
        round_y(nc.vector.tensor_copy, slice(HALF, N))
        for cols in halves:
            quantize_y(cols)
        for q in range(4):
            queue = nc.scalar if q % 2 else nc.sync
            queue.dma_start(
                scales_out[4 * q : 4 * q + 4, :], y_scales[32 * q : 32 * q + 4, :].bitcast(I32)
            )
